import numpy as np, ml_dtypes
CORES = [23,119,17,113]
N = 4
TOK, K = 64, 2
ROUTE = [[[0,2],[1,3],[0,1],[1,2],[0,2],[0,1],[0,1],[0,3],[1,3],[2,3],[0,1],[2,3],[0,1],[1,3],[0,2],[0,3],[1,3],[1,2],[1,2],[1,2],[1,3],[0,1],[1,3],[1,3],[1,2],[0,2],[1,3],[1,2],[0,3],[2,3],[2,3],[0,3],[1,2],[1,3],[0,2],[0,2],[1,3],[2,3],[0,1],[0,3],[1,3],[2,3],[1,3],[2,3],[1,2],[0,3],[0,1],[2,3],[1,2],[1,3],[1,2],[0,2],[0,1],[0,2],[0,2],[0,2],[0,3],[0,2],[1,3],[0,1],[0,3],[0,3],[0,1],[1,3]],[[1,3],[0,1],[0,3],[0,2],[1,2],[0,1],[1,2],[0,3],[0,3],[1,2],[0,2],[0,2],[0,3],[1,3],[0,2],[1,2],[1,2],[0,3],[0,1],[0,2],[1,3],[1,2],[2,3],[0,1],[0,3],[0,1],[1,2],[1,3],[1,2],[0,3],[1,2],[0,2],[0,3],[1,3],[0,1],[0,2],[2,3],[0,2],[0,1],[0,3],[0,3],[2,3],[0,3],[0,3],[1,3],[1,3],[2,3],[0,1],[0,1],[2,3],[0,1],[0,2],[0,1],[0,1],[0,2],[1,3],[0,3],[1,3],[1,2],[0,1],[0,2],[0,2],[0,3],[2,3]],[[0,3],[1,2],[0,3],[1,3],[2,3],[2,3],[0,1],[0,2],[0,3],[1,2],[0,2],[0,2],[0,2],[2,3],[1,3],[0,3],[1,3],[0,2],[0,1],[1,3],[0,3],[0,2],[0,3],[2,3],[2,3],[0,1],[0,3],[0,2],[0,2],[1,2],[0,1],[1,2],[0,1],[0,1],[2,3],[1,3],[2,3],[2,3],[1,2],[1,3],[0,2],[1,3],[1,2],[0,1],[0,2],[0,2],[0,1],[1,2],[0,2],[2,3],[0,2],[0,3],[1,2],[2,3],[0,3],[0,1],[0,1],[1,3],[0,2],[0,1],[0,3],[2,3],[0,2],[0,2]],[[0,3],[0,2],[1,3],[0,1],[1,2],[0,2],[2,3],[1,2],[0,3],[1,2],[1,3],[0,1],[0,1],[0,3],[0,2],[2,3],[0,2],[0,1],[0,1],[1,3],[0,3],[1,2],[2,3],[2,3],[1,3],[0,2],[1,2],[1,2],[0,1],[2,3],[1,2],[2,3],[0,3],[1,2],[0,1],[0,3],[0,1],[0,3],[1,2],[0,2],[0,1],[1,3],[1,2],[1,2],[2,3],[1,2],[0,1],[1,3],[0,3],[1,3],[2,3],[0,1],[0,3],[1,3],[1,2],[0,3],[2,3],[0,1],[2,3],[1,2],[0,2],[0,2],[1,3],[1,2]]]
def setup_inputs(rng):
    rt = (0.75 * rng.standard_normal((128, 1), dtype=np.float32) + rng.standard_normal((128, N), dtype=np.float32) / 2).astype(ml_dtypes.bfloat16)
    rm = np.zeros((N, N, TOK), np.float32)
    for r in range(N):
        for t in range(TOK): rm[r, ROUTE[r][t], t] = 1.0
    return {"x": rng.standard_normal((N, 128, TOK), dtype=np.float32).astype(ml_dtypes.bfloat16), "rt": np.broadcast_to(rt, (N, 128, N)).copy(), "rm": rm.astype(ml_dtypes.bfloat16), "w": rng.standard_normal((N, 128, 128), dtype=np.float32).astype(ml_dtypes.bfloat16)}
def setup_inputs_big(rng):
    d = setup_inputs(rng)
    for k in ("x", "w"): d[k] = (d[k].astype(np.float32) * 1024.0).astype(d[k].dtype)
    return d
def setup_inputs_small(rng):
    d = setup_inputs(rng)
    for k in ("x", "w"): d[k] = (d[k].astype(np.float32) * (1 / 1024.0)).astype(d[k].dtype)
    return d
def setup_inputs_apart(rng):
    d = setup_inputs(rng)
    f = (10.0 ** rng.permutation(np.linspace(-1.5, 1.5, N))).astype(np.float32).reshape(N, 1, 1)
    for k in ("x",): d[k] = (d[k].astype(np.float32) * f).astype(d[k].dtype)
    return d
def setup_inputs_lure(rng):
    d = setup_inputs(rng); x = d["x"].astype(np.float32) * 1024; rt = d["rt"][0].astype(np.float32)
    for r in range(N):
        for t in range(TOK):
            u = int(rng.choice([e for e in range(N) if e not in ROUTE[r][t]]))
            x[r][:, t] += 2097152 * (rt[:, u] - rt[:, ROUTE[r][t][0]])
    d["x"] = x.astype(d["x"].dtype)
    return d
def reference(x, rt, rm, w):
    X, RT, W = x.astype(np.float64), rt.astype(np.float64), w.astype(np.float64)
    y = np.zeros((N, 128, TOK))
    for r in range(N):
        sc = RT[r].T @ X[r]
        for t in range(TOK):
            ex = ROUTE[r][t]; g = np.exp(sc[ex, t] - sc[ex, t].max()); g = g / g.sum()
            y[r][:, t] = sum(g[i] * (W[e].T @ X[r][:, t]) for i, e in enumerate(ex))
    return {"y": y.astype(ml_dtypes.bfloat16)}

@@ -1,0 +1,161 @@
+from concourse.bass import DstId, RemoteDMATransfer
+from concourse.mybir import AluOpType, ActivationFunctionType
+
+N = 4
+TOK = 64
+D = 128
+
+SCRATCH = {
+    "wall": ("sbuf", [128, N * D], "bfloat16"),
+    "xs": ("sbuf", [128, TOK], "bfloat16"),
+    "rts": ("sbuf", [128, N], "bfloat16"),
+    "rms": ("sbuf", [128, TOK], "bfloat16"),
+    "rmrow": ("sbuf", [128, N * TOK], "bfloat16"),
+    "one1": ("sbuf", [128, D], "bfloat16"),
+    "one4": ("sbuf", [128, D], "float32"),
+    "cmat": ("sbuf", [128, N], "float32"),
+    "amat": ("sbuf", [128, N * D], "float32"),
+    "ms": ("sbuf", [128, TOK], "float32"),
+    "xm": ("sbuf", [128, N * TOK], "bfloat16"),
+    "xg": ("sbuf", [128, N * TOK], "bfloat16"),
+    "ysb": ("sbuf", [128, TOK], "bfloat16"),
+    "ps_s": ("psum", [128, 512], "float32"),
+    "ps_rm": ("psum", [128, 512], "float32"),
+    "ps_d0": ("psum", [128, 512], "float32"),
+    "ps_d1": ("psum", [128, 512], "float32"),
+    "ps_d2": ("psum", [128, 512], "float32"),
+    "ps_d3": ("psum", [128, 512], "float32"),
+    "ps_y": ("psum", [128, 512], "float32"),
+}
+SEMAPHORES = (["sw", "sx", "srt", "srm", "srow", "sst", "c1", "cC", "cA", "ss", "sms", "srb", "sxm", "sy", "syc",
+               "sent"]
+              + ["d%d" % e for e in range(N)] + ["q%d" % e for e in range(N)]
+              + ["xg%d" % e for e in range(N)] + ["arr%d" % e for e in range(N)])
+
+
+def _engines(mask):
+    return [i for i in range(mask.bit_length()) if (mask >> i) & 1]
+
+
+def _mask(engines):
+    m = 0
+    for i in engines:
+        m |= 1 << i
+    return m
+
+
+def _plan(src, cores, topo):
+    far = [c for c in cores if c != src and topo.chip(c) != topo.chip(src)]
+    near = [c for c in cores if c != src and topo.chip(c) == topo.chip(src)]
+    plan, used = {}, []
+    if far:
+        av = _engines(topo.mask(src, far[0]))
+        per = len(av) // len(far)
+        for i, c in enumerate(far):
+            plan[c] = _mask(av[i * per:(i + 1) * per])
+            used += av[i * per:(i + 1) * per]
+    if near:
+        av = [i for i in _engines(topo.mask(src, near[0])) if i not in used]
+        per = len(av) // len(near)
+        for i, c in enumerate(near):
+            plan[c] = _mask(av[i * per:(i + 1) * per])
+    return plan, far, near
+
+
+def rank_program(g, core, T, topo):
+    r = T.rank_of(core)
+    if r is None:
+        return
+    S = T.sem
+    cores = list(T.cores)
+    mult = AluOpType.mult
+    v, t, a, sy = g.vector, g.tensor, g.scalar, g.sync
+
+    def wb(e):
+        return T.wall[:, e * D:(e + 1) * D]
+
+    def tb(buf, e):
+        return buf[:, e * TOK:(e + 1) * TOK]
+
+    def dps(e):
+        return T["ps_d%d" % e][:, 0:TOK]
+
+    plan, far, near = _plan(core, cores, topo)
+    order = [r] + [T.rank_of(c) for c in near] + [T.rank_of(c) for c in far]
+
+    sy.dma_start(wb(r), T.w[:]).then_inc(S.sw, 16)
+    a.dma_start(T.xs[:], T.x[:]).then_inc(S.sx, 16)
+    sy.dma_start(T.rts[:], T.rt[:]).then_inc(S.srt, 16)
+    a.dma_start(T.rms[0:N, :], T.rm[:]).then_inc(S.srm, 16)
+    sy.dma_start(T.rmrow[0:1, :], T.rm[:]).then_inc(S.srow, 16)
+
+    v.memset(T.one4[0:N, :], 1.0).then_inc(S.c1, 1)
+    v.memset(T.one1[0:1, :], 1.0).then_inc(S.c1, 1)
+    g.wait_ge(S.c1, 2)
+    g.affine_select(T.cmat[0:N, 0:N], T.one4[0:N, 0:N], [[-1, N]], AluOpType.is_equal, -1.0, 0, 1).then_inc(S.cC, 1)
+    v.wait_ge(S.c1, 2)
+    v.wait_ge(S.cC, 1)
+    for e in range(N):
+        v.tensor_scalar(T.amat[0:N, e * D:(e + 1) * D], T.one4[0:N, :], T.cmat[0:N, e:e + 1], None,
+                        mult).then_inc(S.cA, 1)
+
+    g.wait_ge(S.sw, 16)
+    sent = 0
+    arr = S["arr%d" % r]
+    trs = []
+    for c in far:
+        rid, pid, _ = topo.addr(c)
+        trs.append(RemoteDMATransfer(dst_ids=[DstId(rid=rid, pnc=pid)], dma_engine_mask=plan[c], remote_sem=arr,
+                                     src=wb(r), dst=wb(r)))
+        sent += len(_engines(plan[c]))
+    if trs:
+        g.remote_dma_fused(trs, local_sem=S.sent)
+    for c in near:
+        rid, pid, _ = topo.addr(c)
+        g.remote_dma(wb(r), wb(r), arr, S.sent, pid, rid, plan[c])
+        sent += len(_engines(plan[c]))
+
+    def dmm(e):
+        t.matmul(dps(e), T.amat[0:N, e * D:(e + 1) * D], T.ms[0:N, :], True, True).then_inc(S["d%d" % e], 1)
+
+    t.wait_ge(S.sx, 16)
+    t.wait_ge(S.srt, 16)
+    t.matmul(T.ps_s[0:N, 0:TOK], T.rts[:, 0:N], T.xs[:], True, True).then_inc(S.ss, 1)
+    t.wait_ge(S.sms, 1)
+    t.wait_ge(S.cA, N)
+    dmm(order[0])
+    t.wait_ge(S.srow, 16)
+    t.wait_ge(S.c1, 2)
+    t.matmul(T.ps_rm[:, 0:N * TOK], T.one1[0:1, :], T.rmrow[0:1, :], True, True).then_inc(S.srb, 1)
+    for e in order[1:]:
+        dmm(e)
+
+    v.wait_ge(S.ss, 1)
+    v.wait_ge(S.srm, 16)
+    v.tensor_tensor(T.ms[0:N, :], T.ps_s[0:N, 0:TOK], T.rms[0:N, :], mult).then_inc(S.sms, 1)
+    v.wait_ge(S.srb, 1)
+    v.wait_ge(S.sx, 16)
+    for e in order:
+        v.tensor_tensor(tb(T.xm, e), tb(T.ps_rm, e), T.xs[:], mult).then_inc(S.sxm, 1)
+    v.wait_ge(S.sxm, N)
+
+    for i, e in enumerate(order):
+        a.wait_ge(S["d%d" % e], 1)
+        a.activation(dps(e), dps(e), ActivationFunctionType.Sigmoid).then_inc(S["q%d" % e], 1)
+        v.wait_ge(S["q%d" % e], 1)
+        v.tensor_tensor(tb(T.xg, e), dps(e), tb(T.xm, e), mult).then_inc(S["xg%d" % e], 1)
+        t.wait_ge(S["xg%d" % e], 1)
+        if e == r:
+            t.wait_ge(S.sw, 16)
+        else:
+            t.wait_ge(S["arr%d" % e], len(_engines(_plan(cores[e], cores, topo)[0][core])))
+        mm = t.matmul(T.ps_y[:, 0:TOK], wb(e), tb(T.xg, e), i == 0, i == N - 1)
+        if i == N - 1:
+            mm.then_inc(S.sy, 1)
+
+    v.wait_ge(S.sy, 1)
+    v.tensor_copy(T.ysb[:], T.ps_y[:, 0:TOK]).then_inc(S.syc, 1)
+    sy.wait_ge(S.syc, 1)
+    sy.dma_start(T.y[:], T.ysb[:]).then_inc(S.sst, 16)
+    sy.wait_ge(S.sst, 16)
+    g.wait_ge(S.sent, sent)

@@ -6,31 +6,33 @@ TOK = 64
 D = 128
 
 SCRATCH = {
+    "wst": ("dram", [128, D], "bfloat16"),
     "wall": ("sbuf", [128, N * D], "bfloat16"),
     "xs": ("sbuf", [128, TOK], "bfloat16"),
     "rts": ("sbuf", [128, N], "bfloat16"),
     "rms": ("sbuf", [128, TOK], "bfloat16"),
     "rmrow": ("sbuf", [128, N * TOK], "bfloat16"),
+    "c50": ("sbuf", [128, D], "float32"),
     "one1": ("sbuf", [128, D], "bfloat16"),
-    "one4": ("sbuf", [128, D], "float32"),
-    "cmat": ("sbuf", [128, N], "float32"),
-    "amat": ("sbuf", [128, N * D], "float32"),
+    "one4": ("sbuf", [128, D], "bfloat16"),
+    "pme": ("sbuf", [128, N], "float32"),
+    "idn": ("sbuf", [128, N], "float32"),
+    "chf": ("sbuf", [128, N], "float32"),
+    "sel": ("sbuf", [128, N * D], "bfloat16"),
     "ms": ("sbuf", [128, TOK], "float32"),
+    "gm": ("sbuf", [128, TOK], "bfloat16"),
     "xm": ("sbuf", [128, N * TOK], "bfloat16"),
     "xg": ("sbuf", [128, N * TOK], "bfloat16"),
     "ysb": ("sbuf", [128, TOK], "bfloat16"),
     "ps_s": ("psum", [128, 512], "float32"),
     "ps_rm": ("psum", [128, 512], "float32"),
-    "ps_d0": ("psum", [128, 512], "float32"),
-    "ps_d1": ("psum", [128, 512], "float32"),
-    "ps_d2": ("psum", [128, 512], "float32"),
-    "ps_d3": ("psum", [128, 512], "float32"),
+    "ps_d": ("psum", [128, 512], "float32"),
+    "ps_g": ("psum", [128, 512], "float32"),
     "ps_y": ("psum", [128, 512], "float32"),
 }
-SEMAPHORES = (["sw", "sx", "srt", "srm", "srow", "sst", "c1", "cC", "cA", "ss", "sms", "srb", "sxm", "sy", "syc",
-               "sent"]
-              + ["d%d" % e for e in range(N)] + ["q%d" % e for e in range(N)]
-              + ["xg%d" % e for e in range(N)] + ["arr%d" % e for e in range(N)])
+SEMAPHORES = (["sstg", "sw", "sx", "srt", "srm", "srow", "sst", "c50s", "c1", "sio", "cC", "ssel", "sone", "ss", "sms",
+               "srb", "sxm", "sd", "sgm", "sg", "sxg", "sy", "syc", "sent"]
+              + ["arr%d" % e for e in range(N)])
 
 
 def _engines(mask):
@@ -46,14 +48,12 @@ def _mask(engines):
 
 def _plan(src, cores, topo):
     far = [c for c in cores if c != src and topo.chip(c) != topo.chip(src)]
+    far.sort(key=lambda c: 0 if topo.die(c) != topo.die(src) else 1)
     near = [c for c in cores if c != src and topo.chip(c) == topo.chip(src)]
     plan, used = {}, []
-    if far:
-        av = _engines(topo.mask(src, far[0]))
-        per = len(av) // len(far)
-        for i, c in enumerate(far):
-            plan[c] = _mask(av[i * per:(i + 1) * per])
-            used += av[i * per:(i + 1) * per]
+    for c in far:
+        plan[c] = topo.mask(src, c)
+        used += _engines(plan[c])
     if near:
         av = [i for i in _engines(topo.mask(src, near[0])) if i not in used]
         per = len(av) // len(near)
@@ -70,6 +70,7 @@ def rank_program(g, core, T, topo):
     cores = list(T.cores)
     mult = AluOpType.mult
     v, t, a, sy = g.vector, g.tensor, g.scalar, g.sync
+    Sig = ActivationFunctionType.Sigmoid
 
     def wb(e):
         return T.wall[:, e * D:(e + 1) * D]
@@ -77,74 +78,70 @@ def rank_program(g, core, T, topo):
     def tb(buf, e):
         return buf[:, e * TOK:(e + 1) * TOK]
 
-    def dps(e):
-        return T["ps_d%d" % e][:, 0:TOK]
-
     plan, far, near = _plan(core, cores, topo)
-    order = [r] + [T.rank_of(c) for c in near] + [T.rank_of(c) for c in far]
+    fsend = sorted(far, key=lambda c: 0 if topo.die(c) != topo.die(core) else 1)
+    order = [r] + [T.rank_of(c) for c in near] + [T.rank_of(c) for c in fsend]
 
-    sy.dma_start(wb(r), T.w[:]).then_inc(S.sw, 16)
-    a.dma_start(T.xs[:], T.x[:]).then_inc(S.sx, 16)
-    sy.dma_start(T.rts[:], T.rt[:]).then_inc(S.srt, 16)
+    sy.dma_start(T.wst[:], T.w[:]).then_inc(S.sstg, 16)
     a.dma_start(T.rms[0:N, :], T.rm[:]).then_inc(S.srm, 16)
-    sy.dma_start(T.rmrow[0:1, :], T.rm[:]).then_inc(S.srow, 16)
+    sy.dma_start(T.xs[:], T.x[:]).then_inc(S.sx, 16)
+    a.dma_start(T.rts[:], T.rt[:]).then_inc(S.srt, 16)
+    a.dma_start(T.rmrow[0:1, :], T.rm[:]).then_inc(S.srow, 16)
+    sy.dma_start(wb(r), T.w[:]).then_inc(S.sw, 16)
 
-    v.memset(T.one4[0:N, :], 1.0).then_inc(S.c1, 1)
-    v.memset(T.one1[0:1, :], 1.0).then_inc(S.c1, 1)
-    g.wait_ge(S.c1, 2)
-    g.affine_select(T.cmat[0:N, 0:N], T.one4[0:N, 0:N], [[-1, N]], AluOpType.is_equal, -1.0, 0, 1).then_inc(S.cC, 1)
-    v.wait_ge(S.c1, 2)
-    v.wait_ge(S.cC, 1)
-    for e in range(N):
-        v.tensor_scalar(T.amat[0:N, e * D:(e + 1) * D], T.one4[0:N, :], T.cmat[0:N, e:e + 1], None,
-                        mult).then_inc(S.cA, 1)
-
-    g.wait_ge(S.sw, 16)
+    g.iota(T.pme[0:N, 0:N], [[-1, N]], 0, 1, allow_small_or_imprecise_dtypes=True).then_inc(S.sio, 1)
+    g.wait_ge(S.sstg, 16)
     sent = 0
     arr = S["arr%d" % r]
-    trs = []
-    for c in far:
+    for c in far + near:
         rid, pid, _ = topo.addr(c)
-        trs.append(RemoteDMATransfer(dst_ids=[DstId(rid=rid, pnc=pid)], dma_engine_mask=plan[c], remote_sem=arr,
-                                     src=wb(r), dst=wb(r)))
-        sent += len(_engines(plan[c]))
-    if trs:
-        g.remote_dma_fused(trs, local_sem=S.sent)
-    for c in near:
-        rid, pid, _ = topo.addr(c)
-        g.remote_dma(wb(r), wb(r), arr, S.sent, pid, rid, plan[c])
+        g.remote_dma(wb(r), T.wst[:], arr, S.sent, pid, rid, plan[c])
         sent += len(_engines(plan[c]))
 
-    def dmm(e):
-        t.matmul(dps(e), T.amat[0:N, e * D:(e + 1) * D], T.ms[0:N, :], True, True).then_inc(S["d%d" % e], 1)
+    v.memset(T.c50[0:1, :], 50.0).then_inc(S.c50s, 1)
+    v.memset(T.one4[0:N, :], 1.0).then_inc(S.c1, 1)
+    v.wait_ge(S.sio, 1)
+    v.tensor_scalar(T.idn[0:N, 0:N], T.pme[0:N, 0:N], 0.0, None, AluOpType.is_equal).then_inc(S.cC, 1)
+    v.tensor_scalar(T.chf[0:N, 0:N], T.pme[0:N, 0:N], 0.0, 0.5, AluOpType.is_equal,
+                    AluOpType.subtract).then_inc(S.cC, 1)
+    v.wait_ge(S.c1, 1)
+    v.wait_ge(S.cC, 2)
+    for e in range(N):
+        v.tensor_scalar(T.sel[0:N, e * D:(e + 1) * D], T.one4[0:N, :], T.idn[0:N, e:e + 1], None,
+                        mult).then_inc(S.ssel, 1)
+
+    a.wait_ge(S.c50s, 1)
+    a.activation(T.one1[0:1, :], T.c50[0:1, :], Sig).then_inc(S.sone, 1)
+    a.wait_ge(S.sd, 1)
+    a.activation(T.gm[0:N, :], T.ps_d[0:N, 0:TOK], Sig, scale=2.0).then_inc(S.sgm, 1)
 
     t.wait_ge(S.sx, 16)
     t.wait_ge(S.srt, 16)
     t.matmul(T.ps_s[0:N, 0:TOK], T.rts[:, 0:N], T.xs[:], True, True).then_inc(S.ss, 1)
     t.wait_ge(S.sms, 1)
-    t.wait_ge(S.cA, N)
-    dmm(order[0])
+    t.wait_ge(S.cC, 2)
+    t.matmul(T.ps_d[0:N, 0:TOK], T.chf[0:N, 0:N], T.ms[0:N, :], True, True).then_inc(S.sd, 1)
     t.wait_ge(S.srow, 16)
-    t.wait_ge(S.c1, 2)
+    t.wait_ge(S.sone, 1)
     t.matmul(T.ps_rm[:, 0:N * TOK], T.one1[0:1, :], T.rmrow[0:1, :], True, True).then_inc(S.srb, 1)
-    for e in order[1:]:
-        dmm(e)
+    t.wait_ge(S.sgm, 1)
+    t.wait_ge(S.ssel, N)
+    for e in range(N):
+        t.matmul(tb(T.ps_g, e), T.sel[0:N, e * D:(e + 1) * D], T.gm[0:N, :], True, True).then_inc(S.sg, 1)
 
     v.wait_ge(S.ss, 1)
     v.wait_ge(S.srm, 16)
     v.tensor_tensor(T.ms[0:N, :], T.ps_s[0:N, 0:TOK], T.rms[0:N, :], mult).then_inc(S.sms, 1)
     v.wait_ge(S.srb, 1)
     v.wait_ge(S.sx, 16)
-    for e in order:
+    for e in range(N):
         v.tensor_tensor(tb(T.xm, e), tb(T.ps_rm, e), T.xs[:], mult).then_inc(S.sxm, 1)
     v.wait_ge(S.sxm, N)
+    v.wait_ge(S.sg, N)
+    v.tensor_tensor(T.xg[:], T.ps_g[:, 0:N * TOK], T.xm[:], mult).then_inc(S.sxg, 1)
 
+    t.wait_ge(S.sxg, 1)
     for i, e in enumerate(order):
-        a.wait_ge(S["d%d" % e], 1)
-        a.activation(dps(e), dps(e), ActivationFunctionType.Sigmoid).then_inc(S["q%d" % e], 1)
-        v.wait_ge(S["q%d" % e], 1)
-        v.tensor_tensor(tb(T.xg, e), dps(e), tb(T.xm, e), mult).then_inc(S["xg%d" % e], 1)
-        t.wait_ge(S["xg%d" % e], 1)
         if e == r:
             t.wait_ge(S.sw, 16)
         else:

from concourse.bass import DstId, RemoteDMATransfer
from concourse.mybir import AluOpType, ActivationFunctionType

N = 4
TOK = 64
D = 128

SCRATCH = {
    "wst": ("dram", [128, D], "bfloat16"),
    "wall": ("sbuf", [128, N * D], "bfloat16"),
    "xs": ("sbuf", [128, TOK], "bfloat16"),
    "rts": ("sbuf", [128, N], "bfloat16"),
    "rms": ("sbuf", [128, TOK], "bfloat16"),
    "rmrow": ("sbuf", [128, N * TOK], "bfloat16"),
    "c50": ("sbuf", [128, D], "float32"),
    "one1": ("sbuf", [128, D], "bfloat16"),
    "one4": ("sbuf", [128, D], "bfloat16"),
    "pme": ("sbuf", [128, N], "float32"),
    "idn": ("sbuf", [128, N], "float32"),
    "chf": ("sbuf", [128, N], "float32"),
    "sel": ("sbuf", [128, N * D], "bfloat16"),
    "ms": ("sbuf", [128, TOK], "float32"),
    "gm": ("sbuf", [128, TOK], "bfloat16"),
    "xm": ("sbuf", [128, N * TOK], "bfloat16"),
    "xg": ("sbuf", [128, N * TOK], "bfloat16"),
    "ysb": ("sbuf", [128, TOK], "bfloat16"),
    "ps_s": ("psum", [128, 512], "float32"),
    "ps_rm": ("psum", [128, 512], "float32"),
    "ps_d": ("psum", [128, 512], "float32"),
    "ps_g": ("psum", [128, 512], "float32"),
    "ps_y": ("psum", [128, 512], "float32"),
}
SEMAPHORES = (["sstg", "sw", "sx", "srt", "srm", "srow", "sst", "c50s", "c1", "sio", "cC", "ssel", "sone", "ss", "sms",
               "srb", "sxm", "sd", "sgm", "sg", "sxg", "sy", "syc", "sent"]
              + ["arr%d" % e for e in range(N)])


def _engines(mask):
    return [i for i in range(mask.bit_length()) if (mask >> i) & 1]


def _mask(engines):
    m = 0
    for i in engines:
        m |= 1 << i
    return m


def _plan(src, cores, topo):
    far = [c for c in cores if c != src and topo.chip(c) != topo.chip(src)]
    far.sort(key=lambda c: 0 if topo.die(c) != topo.die(src) else 1)
    near = [c for c in cores if c != src and topo.chip(c) == topo.chip(src)]
    plan, used = {}, []
    for c in far:
        plan[c] = topo.mask(src, c)
        used += _engines(plan[c])
    if near:
        av = [i for i in _engines(topo.mask(src, near[0])) if i not in used]
        per = len(av) // len(near)
        for i, c in enumerate(near):
            plan[c] = _mask(av[i * per:(i + 1) * per])
    return plan, far, near


def rank_program(g, core, T, topo):
    r = T.rank_of(core)
    if r is None:
        return
    S = T.sem
    cores = list(T.cores)
    mult = AluOpType.mult
    v, t, a, sy = g.vector, g.tensor, g.scalar, g.sync
    Sig = ActivationFunctionType.Sigmoid

    def wb(e):
        return T.wall[:, e * D:(e + 1) * D]

    def tb(buf, e):
        return buf[:, e * TOK:(e + 1) * TOK]

    plan, far, near = _plan(core, cores, topo)
    fsend = sorted(far, key=lambda c: 0 if topo.die(c) != topo.die(core) else 1)
    order = [r] + [T.rank_of(c) for c in near] + [T.rank_of(c) for c in fsend]

    sy.dma_start(T.wst[:], T.w[:]).then_inc(S.sstg, 16)
    a.dma_start(T.rms[0:N, :], T.rm[:]).then_inc(S.srm, 16)
    sy.dma_start(T.xs[:], T.x[:]).then_inc(S.sx, 16)
    a.dma_start(T.rts[:], T.rt[:]).then_inc(S.srt, 16)
    a.dma_start(T.rmrow[0:1, :], T.rm[:]).then_inc(S.srow, 16)
    sy.dma_start(wb(r), T.w[:]).then_inc(S.sw, 16)

    g.iota(T.pme[0:N, 0:N], [[-1, N]], 0, 1, allow_small_or_imprecise_dtypes=True).then_inc(S.sio, 1)
    g.wait_ge(S.sstg, 16)
    sent = 0
    arr = S["arr%d" % r]
    for c in far + near:
        rid, pid, _ = topo.addr(c)
        g.remote_dma(wb(r), T.wst[:], arr, S.sent, pid, rid, plan[c])
        sent += len(_engines(plan[c]))

    v.memset(T.c50[0:1, :], 50.0).then_inc(S.c50s, 1)
    v.memset(T.one4[0:N, :], 1.0).then_inc(S.c1, 1)
    v.wait_ge(S.sio, 1)
    v.tensor_scalar(T.idn[0:N, 0:N], T.pme[0:N, 0:N], 0.0, None, AluOpType.is_equal).then_inc(S.cC, 1)
    v.tensor_scalar(T.chf[0:N, 0:N], T.pme[0:N, 0:N], 0.0, 0.5, AluOpType.is_equal,
                    AluOpType.subtract).then_inc(S.cC, 1)
    v.wait_ge(S.c1, 1)
    v.wait_ge(S.cC, 2)
    for e in range(N):
        v.tensor_scalar(T.sel[0:N, e * D:(e + 1) * D], T.one4[0:N, :], T.idn[0:N, e:e + 1], None,
                        mult).then_inc(S.ssel, 1)

    a.wait_ge(S.c50s, 1)
    a.activation(T.one1[0:1, :], T.c50[0:1, :], Sig).then_inc(S.sone, 1)
    a.wait_ge(S.sd, 1)
    a.activation(T.gm[0:N, :], T.ps_d[0:N, 0:TOK], Sig, scale=2.0).then_inc(S.sgm, 1)

    t.wait_ge(S.sx, 16)
    t.wait_ge(S.srt, 16)
    t.matmul(T.ps_s[0:N, 0:TOK], T.rts[:, 0:N], T.xs[:], True, True).then_inc(S.ss, 1)
    t.wait_ge(S.sms, 1)
    t.wait_ge(S.cC, 2)
    t.matmul(T.ps_d[0:N, 0:TOK], T.chf[0:N, 0:N], T.ms[0:N, :], True, True).then_inc(S.sd, 1)
    t.wait_ge(S.srow, 16)
    t.wait_ge(S.sone, 1)
    t.matmul(T.ps_rm[:, 0:N * TOK], T.one1[0:1, :], T.rmrow[0:1, :], True, True).then_inc(S.srb, 1)
    t.wait_ge(S.sgm, 1)
    t.wait_ge(S.ssel, N)
    for e in range(N):
        t.matmul(tb(T.ps_g, e), T.sel[0:N, e * D:(e + 1) * D], T.gm[0:N, :], True, True).then_inc(S.sg, 1)

    v.wait_ge(S.ss, 1)
    v.wait_ge(S.srm, 16)
    v.tensor_tensor(T.ms[0:N, :], T.ps_s[0:N, 0:TOK], T.rms[0:N, :], mult).then_inc(S.sms, 1)
    v.wait_ge(S.srb, 1)
    v.wait_ge(S.sx, 16)
    for e in range(N):
        v.tensor_tensor(tb(T.xm, e), tb(T.ps_rm, e), T.xs[:], mult).then_inc(S.sxm, 1)
    v.wait_ge(S.sxm, N)
    v.wait_ge(S.sg, N)
    v.tensor_tensor(T.xg[:], T.ps_g[:, 0:N * TOK], T.xm[:], mult).then_inc(S.sxg, 1)

    t.wait_ge(S.sxg, 1)
    for i, e in enumerate(order):
        if e == r:
            t.wait_ge(S.sw, 16)
        else:
            t.wait_ge(S["arr%d" % e], len(_engines(_plan(cores[e], cores, topo)[0][core])))
        mm = t.matmul(T.ps_y[:, 0:TOK], wb(e), tb(T.xg, e), i == 0, i == N - 1)
        if i == N - 1:
            mm.then_inc(S.sy, 1)

    v.wait_ge(S.sy, 1)
    v.tensor_copy(T.ysb[:], T.ps_y[:, 0:TOK]).then_inc(S.syc, 1)
    sy.wait_ge(S.syc, 1)
    sy.dma_start(T.y[:], T.ysb[:]).then_inc(S.sst, 16)
    sy.wait_ge(S.sst, 16)
    g.wait_ge(S.sent, sent)
